import numpy as np, ml_dtypes
CORES = [17,57,65,89,97,121]
N = 6
S, B = 2, 512
def setup_inputs(rng):
    return {"x": rng.standard_normal((N, 128, S * B), dtype=np.float32).astype(ml_dtypes.bfloat16), "gate": (0.9375 + 0.03125 * rng.standard_normal((N, 128, S * B), dtype=np.float32)).astype(ml_dtypes.bfloat16)}
def setup_inputs_big(rng):
    d = setup_inputs(rng)
    for k in ("x",): d[k] = (d[k].astype(np.float32) * 1048576.0).astype(d[k].dtype)
    return d
def setup_inputs_small(rng):
    d = setup_inputs(rng)
    for k in ("x",): d[k] = (d[k].astype(np.float32) * (1 / 1048576.0)).astype(d[k].dtype)
    return d
def setup_inputs_apart(rng):
    d = setup_inputs(rng)
    f = (10.0 ** rng.permutation(np.linspace(-1.5, 1.5, N))).astype(np.float32).reshape(N, 1, 1)
    for k in ("x",): d[k] = (d[k].astype(np.float32) * f).astype(d[k].dtype)
    return d
def reference(x, gate):
    X, GATE = x.astype(np.float64), gate.astype(np.float64)
    y = np.zeros((N, 128, S * B)); h = np.zeros((128, B))
    for r in range(N):
        for s in range(S):
            h = GATE[r][:, B * s:B * s + B] * h + X[r][:, B * s:B * s + B]
            y[r][:, B * s:B * s + B] = h
    return {"y": y.astype(ml_dtypes.bfloat16)}

from concourse.bass import DstId, RemoteDMATransfer
from concourse.mybir import AluOpType

N, B = 6, 512
W = 4
C = B // W
NV = 40

SCRATCH = {
    "gs": ("sbuf", [128, 2 * B], "bfloat16"),
    "xs": ("sbuf", [128, 2 * B], "bfloat16"),
    "sb": ("sbuf", [128, W * 2 * C], "bfloat16"),
    "fb": ("sbuf", [128, W * 2 * C], "bfloat16"),
    "cb": ("sbuf", [128, 5 * 2 * C], "bfloat16"),
    "hb": ("sbuf", [128, 4 * C], "bfloat16"),
    "hin": ("sbuf", [128, B], "bfloat16"),
    "yb": ("sbuf", [128, 2 * B], "bfloat16"),
    "p0": ("psum", [128, B], "float32"),
    "p1": ("psum", [128, B], "float32"),
    "p2": ("psum", [128, B], "float32"),
    "p3": ("psum", [128, B], "float32"),
    "p4": ("psum", [128, B], "float32"),
    "p5": ("psum", [128, B], "float32"),
}
SEMAPHORES = (["ldg", "ldx", "st", "sent"] + ["fw%d" % k for k in range(W)] + ["arr%d" % r for r in range(5)]
              + ["hs%d" % k for k in range(W)] + ["v%d" % i for i in range(NV)])


def _bits(m):
    return [b for b in range(m.bit_length()) if (m >> b) & 1]


def _pick(bits, lo, n):
    return sum(1 << b for b in bits[lo:lo + n])


def _plan(T, topo):
    cores = list(T.cores)
    port = []
    for rc in cores:
        cand = [k for k in range(topo.CHIPS * topo.CORES_PER_CHIP)
                if topo.chip(k) == topo.chip(rc) and topo.die(k) == topo.die(rc) and k not in cores
                and all(topo.may_write(k, d) for d in cores)]
        port.append(cand[0])
    return cores, port, [port[k + 1] for k in range(W)]


def rank_program(g, core, T, topo):
    cores, port, workers = _plan(T, topo)
    rank = T.rank_of(core)
    if rank is None and core not in port[:5]:
        return
    V = g.vector
    mult, add = AluOpType.mult, AluOpType.add
    m = None
    for d in cores + port:
        if d != core:
            m = topo.mask(core, d) if m is None else m & topo.mask(core, d)
    eng = _bits(m)
    NE = len(eng)
    HE = NE // 2
    sent = [0]
    nv = [0]

    def vop(ins):
        s = T.sem["v%d" % nv[0]]
        nv[0] += 1
        ins.then_inc(s, 1)
        return s

    def write(dst, out, src, sem):
        rid, pid, _ = topo.addr(dst)
        g.remote_dma(out, src, sem, T.sem.sent, pid, rid, _pick(eng, 0, NE))
        sent[0] += NE

    def part(r):
        return C if r == 0 else 0

    def direct(r, k):
        return topo.may_write(cores[r], workers[k])

    if rank is None:
        r = port.index(core)
        for k in [k for k in range(W) if not direct(r, k)]:
            g.wait_ge(T.sem["fw%d" % k], NE)
            write(workers[k], T.cb[:, r * 2 * C + part(r):(r + 1) * 2 * C],
                  T.fb[:, k * 2 * C + part(r):(k + 1) * 2 * C], T.sem["arr%d" % r])
        if core in workers:
            k = workers.index(core)
            early = [q for q in range(5) if direct(q, k)]
            arr = [T.sem["arr%d" % q] for q in range(5)]
            b0 = T.cb[:, C:2 * C]
            pre = {}
            for q in early:
                if q == 0 and 1 in early:
                    continue
                V.wait_ge(arr[q], NE)
                if q == 0:
                    pre[0] = (T.p1[:, 0:C], vop(V.tensor_copy(T.p1[:, 0:C], b0)))
                else:
                    o = T.p0[:, (q - 1) * C:q * C]
                    pre[q] = (o, vop(V.tensor_copy(o, T.cb[:, q * 2 * C:q * 2 * C + C])))
            for q in pre:
                V.wait_ge(pre[q][1], 1)
            h, hsem = b0, []
            V.wait_ge(arr[0], NE)
            for q in range(1, 5):
                V.wait_ge(arr[q], NE)
                a = T.cb[:, q * 2 * C:q * 2 * C + C]
                if q in pre:
                    in0, in1 = pre[q][0], h
                elif q == 1 and 0 in pre:
                    in0, in1 = pre[0][0], a
                else:
                    in0, in1 = a, h
                mp = T.p2[:, (q - 1) * C:q * C]
                V.wait_ge(vop(V.tensor_tensor(mp, in0, in1, mult)), 1)
                h = T.hb[:, (q - 1) * C:q * C]
                s = vop(V.tensor_tensor(h, mp, T.cb[:, q * 2 * C + C:(q + 1) * 2 * C], add))
                hsem.append(s)
                if q < 4:
                    V.wait_ge(s, 1)
            land = T.hin[:, k * C:(k + 1) * C]
            hs = T.sem["hs%d" % k]
            g.wait_ge(arr[0], NE)
            write(cores[1], land, b0, hs)
            for q in (2, 4):
                g.wait_ge(hsem[q - 2], 1)
                g.wait_ge(hsem[q - 1], 1)
                tr = []
                for j in (0, 1):
                    rid, pid, _ = topo.addr(cores[q + j])
                    tr.append(RemoteDMATransfer(dst_ids=[DstId(rid=rid, pnc=pid)],
                                                dma_engine_mask=_pick(eng, j * HE, HE), remote_sem=hs,
                                                src=T.hb[:, (q + j - 2) * C:(q + j - 1) * C], dst=land))
                g.remote_dma_fused(tr, local_sem=T.sem.sent)
                sent[0] += 2 * HE
        g.wait_ge(T.sem.sent, sent[0])
        return

    r = rank
    g.sync.dma_start(T.gs[:], T.gate[:]).then_inc(T.sem.ldg, 16)
    g.scalar.dma_start(T.xs[:], T.x[:]).then_inc(T.sem.ldx, 16)
    order = [k for k in range(W) if not direct(r, k)] + [k for k in range(W) if direct(r, k)]
    nst = 0

    def c0(k):
        return slice(k * C, (k + 1) * C)

    def c1(k):
        return slice(B + k * C, B + (k + 1) * C)

    def send(k, src):
        if direct(r, k):
            write(workers[k], T.cb[:, r * 2 * C + part(r):(r + 1) * 2 * C], src, T.sem["arr%d" % r])
        else:
            write(port[r], T.fb[:, k * 2 * C + part(r):(k + 1) * 2 * C], src, T.sem["fw%d" % k])

    V.wait_ge(T.sem.ldg, 16)
    if r == 0:
        V.wait_ge(T.sem.ldx, 16)
        sB = []
        for k in order:
            V.wait_ge(vop(V.tensor_tensor(T.p1[:, c0(k)], T.gs[:, c1(k)], T.xs[:, c0(k)], mult)), 1)
            s = vop(V.tensor_tensor(T.yb[:, c1(k)], T.p1[:, c0(k)], T.xs[:, c1(k)], add))
            sB.append(s)
            g.wait_ge(s, 1)
            send(k, T.yb[:, c1(k)])
        g.sync.wait_ge(T.sem.ldx, 16)
        g.sync.dma_start(T.y[:, 0:B], T.xs[:, 0:B]).then_inc(T.sem.st, 16)
        for s in sB:
            g.scalar.wait_ge(s, 1)
        g.scalar.dma_start(T.y[:, B:2 * B], T.yb[:, B:2 * B]).then_inc(T.sem.st, 16)
        g.wait_ge(T.sem.sent, sent[0])
        g.wait_ge(T.sem.st, 32)
        return

    sB = {}
    for i, k in enumerate(order):
        V.wait_ge(vop(V.tensor_copy(T.p0[:, c0(k)], T.gs[:, c1(k)])), 1)
        if r < 5:
            sA = vop(V.tensor_tensor(T.sb[:, k * 2 * C:k * 2 * C + C], T.p0[:, c0(k)], T.gs[:, c0(k)], mult))
        if i == 0:
            V.wait_ge(T.sem.ldx, 16)
        V.wait_ge(vop(V.tensor_tensor(T.p1[:, c0(k)], T.p0[:, c0(k)], T.xs[:, c0(k)], mult)), 1)
        sB[k] = vop(V.tensor_tensor(T.sb[:, k * 2 * C + C:(k + 1) * 2 * C], T.p1[:, c0(k)], T.xs[:, c1(k)], add))
        if r < 5:
            g.wait_ge(sA, 1)
            g.wait_ge(sB[k], 1)
            send(k, T.sb[:, k * 2 * C:(k + 1) * 2 * C])
    sPA = vop(V.tensor_tensor(T.p2[:], T.p0[:], T.gs[:, 0:B], mult))
    sPG = vop(V.tensor_copy(T.p3[:], T.gs[:, 0:B]))
    V.wait_ge(sPA, 1)
    V.wait_ge(sPG, 1)
    for k in range(W):
        V.wait_ge(sB[k], 1)
    for k in range(W):
        V.wait_ge(T.sem["hs%d" % k], NE if r == 1 else HE)
        a = vop(V.tensor_tensor(T.p4[:, c0(k)], T.p3[:, c0(k)], T.hin[:, c0(k)], mult))
        b = vop(V.tensor_tensor(T.p5[:, c0(k)], T.p2[:, c0(k)], T.hin[:, c0(k)], mult))
        V.wait_ge(a, 1)
        s0 = vop(V.tensor_tensor(T.yb[:, c0(k)], T.p4[:, c0(k)], T.xs[:, c0(k)], add))
        V.wait_ge(b, 1)
        s1 = vop(V.tensor_tensor(T.yb[:, c1(k)], T.p5[:, c0(k)], T.sb[:, k * 2 * C + C:(k + 1) * 2 * C], add))
        g.sync.wait_ge(s0, 1)
        g.sync.dma_start(T.y[:, c0(k)], T.yb[:, c0(k)]).then_inc(T.sem.st, 16)
        g.scalar.wait_ge(s1, 1)
        g.scalar.dma_start(T.y[:, c1(k)], T.yb[:, c1(k)]).then_inc(T.sem.st, 16)
        nst += 2
    if sent[0]:
        g.wait_ge(T.sem.sent, sent[0])
    g.wait_ge(T.sem.st, 16 * nst)
